import numpy as np, ml_dtypes
CORES = [25,29,65,69,153,157,193,197]
N = 8
import mx_ref
BF = ml_dtypes.bfloat16
def gcols(t, e):
    v = np.concatenate([t.reshape(8, 16, -1, 4), np.zeros((8, 16, 1, 4), BF)], axis=2)
    return np.ascontiguousarray(np.stack([v[g][:, e[g]] for g in range(8)])).reshape(128, -1)
def tile(rs):
    return np.stack(rs, axis=2).reshape(128, -1).astype(BF)
def pick(q, e):
    c = np.concatenate([q[0].reshape(128, -1, 4), np.zeros((128, 1, 4), np.uint8)], axis=1); s = np.concatenate([q[1], np.ones((16, 1), np.uint8)], axis=1)
    return (np.ascontiguousarray(c[:, e].reshape(128, -1)), np.ascontiguousarray(s[:, e]))
def join(*qs):
    return (np.concatenate([q[0] for q in qs], axis=1), np.concatenate([q[1] for q in qs], axis=1))
def put(q, e, v):
    c, s = q[0].reshape(128, -1, 4).copy(), q[1].copy(); c[:, e] = v[0].reshape(128, -1, 4); s[:, e] = v[1]
    return (c.reshape(128, -1), s)
def pk(c, s):
    return (np.ascontiguousarray(c), mx_ref.live(s))
def emit(q):
    return q[0], q[1]
def packed(v, rng):
    q = [mx_ref.quantize(np.ascontiguousarray(v[r])) for r in range(N)]
    return np.stack([a for a, b in q]), np.stack([mx_ref.plane(b, rng) for a, b in q])
def values_of_codes():
    e, c = np.zeros((128, 128, 4), np.float32), np.zeros((128, 2, 4), np.uint8)
    e[np.arange(128), np.arange(128), 0] = 1
    c[:127, :, 0] = np.arange(256).reshape(2, 128).T[:127]
    return mx_ref.matmul(mx_ref.quantize(e.reshape(128, 512).astype(BF)), (c.reshape(128, 8), np.full((16, 2), 127, np.uint8))).T.reshape(-1).astype(np.float64)
CODE_VALUE, SCALE_VALUE = values_of_codes(), 2.0 ** (np.arange(256) - 127.0)
def decode(q):
    return (CODE_VALUE[q[0]].reshape(16, 8, -1, 4) * SCALE_VALUE[q[1]][:, None, :, None] + 0.0).reshape(128, -1).astype(np.float32)
def f(rng, *shape):
    return mx_ref.flush((rng.standard_normal(shape, dtype=np.float32) * np.exp2(rng.integers(-2, 3, shape[:-1] + (1,)))).astype(BF))
def wide(rng, *shape, cols=0):
    v = rng.standard_normal(shape, dtype=np.float32) * np.exp2(rng.integers(-12, 13, shape)).astype(np.float32)
    if cols: v *= np.repeat(np.exp2(rng.integers(-cols, cols + 1, shape[:-2] + (1, shape[-1] // 4))) * (rng.random(shape[:-2] + (1, shape[-1] // 4)) > 0.0625), 4, axis=-1).astype(np.float32)
    return mx_ref.flush(v.astype(BF))
C, A, STEP = 256, 14, [4, 1]
def big(v):
    v = v.astype(np.float32)
    v[np.abs(v) < np.float32(2.0 ** -16)] = 0
    return v.astype(BF)
def numbers_of(rng):
    return {"x": big(f(rng, N, 128, 4 * C)), "u": np.array(f(rng, N, 128, 512)), "v": np.array(f(rng, N, 128, 512))}
def layers(rng):
    return big(rng.random((N, 128, 2048), dtype=np.float32) * 2 - 1).reshape(N, 8, 16, 4, 8, 16, 4)
def weights(rng, w):
    c, s = packed(np.ascontiguousarray(w).reshape(N, 128, 2048), rng)
    return {"wc": c, "ws": s}
def setup_inputs(rng):
    return {**numbers_of(rng), **weights(rng, layers(rng))}
def setup_inputs_ties(rng):
    d = numbers_of(rng)
    o = rng.permutation(N)
    x = d["x"].reshape(N, 8, 16, C, 4)
    x[:, :, :8] = 0
    x[:, :, 0, :, 0] = rng.integers(0, 4, (N, 8, C)).astype(np.float32).astype(BF)
    t = rng.integers(-1, 2, (N, 8, C, 3))
    t[o[0]] = -1
    t[o[0], :, A::A + 1, 0] = 1
    t[o[1]] = 1
    x[:, :, 1, :, :3] = t.astype(np.float32).astype(BF)
    u = d["u"].reshape(N, 128, 128, 4)
    for i in range(4): u[:, :, i::16] = 0
    for r in range(N):
        for h in range(0, 128, 16):
            u[r, h, h, 0] = 0.0 if r == o[0] else -1.0 if r == o[2] else 1.0
            for i in range(3): u[r, h + 1, h + 1 + i, i] = 1.0
    w = layers(rng)
    w[:, :, :, :, :, :8] = 0
    return {"x": x.reshape(N, 128, 4 * C), "u": u.reshape(N, 128, 512), "v": d["v"], **weights(rng, w)}
def setup_inputs_near(rng):
    d = numbers_of(rng)
    x = d["x"].astype(np.float32).reshape(N, 8, 16, C, 4)
    x[:, :, 0] = 0
    x[:, :, 8:] = 0
    u = d["u"].reshape(N, 128, 128, 4)
    for i in range(4): u[:, :, i::16] = 0
    o = rng.permutation(N) % 4
    for r in range(N):
        tiny = o[r] == 2
        k = 2.0 ** -30 if o[r] == 1 else 1.0
        if tiny:
            m = rng.integers(0, 8, (8, C))
            x[r, :, 8, :, 0] = (8 + m) * 2.0 ** -33
            x[r, :, 9, :, 0] = (15 - m) * 2.0 ** -33
        else:
            s = rng.integers(0, 16, (8, C))
            x[r, :, 0, :, 0] = 1.0 if o[r] == 0 else -1.0 if o[r] == 1 else rng.choice([-1.0, 1.0], (8, C))
            x[r, :, 8] = ((s[:, :, None] >> np.arange(4)) & 1) * np.exp2(np.arange(4) - 23.0)
            x[r, :, 11, :, 0] = 2.0 ** -10
        x[r, :, 12:15, :, 0] = rng.integers(-1, 2, (8, 3, C)) * (2.0 ** -30 if tiny else 2.0 ** -22)
        if o[r] in (0, 2):
            for g in rng.permutation(8)[:4]: x[r, g, 0, rng.integers(C), 1] = rng.choice([-1.0, 1.0]) * 2.0 ** 21
        for h in range(0, 128, 16):
            if tiny:
                u[r, h + 8, h, 0] = 1.125 * 2.0 ** -30
                u[r, h + 9, h, 0] = 2.0 ** -30
            else:
                u[r, h, h, 0] = k
                u[r, h + 8, h] = k
                u[r, h + 11, h, 0] = k
            if o[r] in (0, 2): u[r, h, h, 1] = 2.0 ** 9
            for i in range(3): u[r, h + 12 + i, h + 1 + i, 0] = 2.0 ** -30
    w = layers(rng)
    for i in [0, 8, 9, 10, 11, 12, 13, 14, 15]:
        w[:, :, i] = 0
        w[:, :, :, :, :, i] = 0
    return {"x": x.reshape(N, 128, 4 * C).astype(BF), "u": u.reshape(N, 128, 512), "v": d["v"], **weights(rng, w)}
def setup_inputs_ends(rng):
    d = numbers_of(rng)
    e = rng.permutation(N)
    top = e[0] ^ STEP[0] ^ STEP[1]
    mate = top ^ STEP[0]
    rest = [r for r in e[1:] if r not in (top, mate)]
    e = [e[0]] + rest[:N // 2 - 1] + [top, mate] + rest[N // 2 - 1:]
    c = rng.integers(8)
    x = np.zeros((N, 8, 16, C, 4), np.float32)
    u = d["u"].astype(np.float32).reshape(N, 8, 16, 128, 4)
    for i in range(4): u[:, :, :, i::16] = 0
    v = rng.choice([-1.0, 1.0], (N, 128, 512)).astype(np.float32)
    sign = lambda *s: rng.choice([-1.0, 1.0], s)
    for r in range(N):
        h = rng.permutation(8)
        if r in e[:N // 2]:
            t = sign(4, 1, 1, 1)
            if r == e[0]: t[:] = -1
            m = sign(8, 1, C, 1) * rng.choice([0.5, 0.75, 0.875, 1.0], (8, 1, C, 1))
            m[h[4:, None], 0, rng.permutation(C)[:64], 0] = -rng.choice([0.75, 0.875, 1.0], (4, 64))
            p = (m[h[4:]] > 0).all(axis=0)
            m[h[4]][p] *= -1
            m[h[:4]] = t
            x[r] = 2.0 ** 21 * m
            v[r] *= np.float32(2.0 ** 30)
            for n in range(8):
                g = h[n]
                if n < 4: u[r, h[:4], :, 16 * g] = -2.0 ** 30 * t[:, :, 0]
                if n in (2, 3): u[r, h[4:], :, 16 * g] = 2.0 ** 29 if n == 2 else 2.0 ** 30
                if n >= 4: u[r, h[4:], :, 16 * g] = 2.0 ** 30 * sign(4, 1, 1)
                for i in range(3): u[r, rng.choice(h[4:]), :, 16 * g + 1 + i] = 2.0 ** 30 * rng.choice([-1.0, 1.0])
        elif r == top:
            x[r] = 2.0 ** 21
            s = (rng.permutation(C)[:, None] >> np.arange(8)) & 1
            x[r, c, :2] = 2.0 ** 21 * (2.0 * s - 1.0).reshape(C, 2, 4).transpose(1, 0, 2)
            v[r] *= np.float32(2.0 ** 30)
            for n in range(8):
                g = h[n]
                u[r, :, :, 16 * g] = -2.0 ** 30 if n < 4 else 2.0 ** 30
                k = 4.0 * rng.permutation(2)[:, None] + rng.permutation(4)
                u[r, c, :2, 16 * g] *= np.exp2(-k).astype(np.float32)
        else:
            x[r, :, :8] = 2.0 ** -30 * sign(8, 1, C, 1)
            x[r, :, 8:] = sign(8, 1, C, 1)
            v[r] *= np.float32(2.0 ** -30)
            for n in range(8):
                g = h[n]
                if n >= 2: u[r, :, :8, 16 * g] = 2.0 ** -30 * sign(8, 1, 1)
                for i in range(3): u[r, rng.integers(8), :8, 16 * g + 1 + i] = 2.0 ** -30 * rng.choice([-1.0, 1.0])
    w = rng.choice([-1.0, 1.0], (N, 8, 16, 4, 8, 16, 4)).astype(np.float32)
    w[e[0]] = 1
    w[e[1]] = 0
    w[:, :, :8] = 0
    w[:, :, :, :, :, :8] = 0
    w[mate] = 1
    w[mate, c, :2] = 0
    return {"x": x.reshape(N, 128, 4 * C).astype(BF), "u": u.reshape(N, 128, 512).astype(BF), "v": v.astype(BF), **weights(rng, w.astype(BF))}
def setup_inputs_blocks(rng):
    d = numbers_of(rng)
    k = np.exp2(rng.integers(14, 19, (N, 8, 2, 1, C, 1)).astype(np.float64))
    s = (N, 8, 2, 8, C, 4)
    a = k * np.exp2(-rng.integers(8, 15, s).astype(np.float64)) * (1 + (2 * rng.integers(0, 64, s) + 1) * 2.0 ** -7) * rng.choice([-1.0, 1.0], s)
    a[:, :, :, 0, :, 0] = 1.96875 * k[:, :, :, 0, :, 0] * rng.choice([-1.0, 1.0], (N, 8, 2, C))
    u = d["u"].reshape(N, 128, 128, 4)
    e = rng.integers(N)
    for i in range(4): u[e, :, i::16] = 0
    w = layers(rng)
    w[:, :, ::8] = 0
    return {"x": a.astype(np.float32).reshape(N, 128, 4 * C).astype(BF), "u": u.reshape(N, 128, 512), "v": d["v"], **weights(rng, w)}
def setup_inputs_spread(rng):
    d = setup_inputs(rng)
    d["x"] = big(np.clip(wide(rng, N, 128, 4 * C, cols=6).astype(np.float32), -2.0 ** 21, 2.0 ** 21))
    return d
def check_inputs(d):
    b = []
    for k, top in (("x", 2.0 ** 21), ("u", 2.0 ** 30), ("v", 2.0 ** 30)):
        a = np.abs(d[k].astype(np.float32))
        if not (np.isfinite(a).all() and ((a == 0) | (a >= 2.0 ** -30) & (a <= top)).all()): b.append("a value of " + k)
    none, least, most = [emit(mx_ref.quantize(np.full((128, 16), k, np.float32).astype(BF)))[1][0, 0] for k in (0.0, 2.0 ** -30, 1.0)]
    for r in range(N):
        if ((d["wc"][r] == 0x7F) | (d["wc"][r] == 0xFF)).any(): b.append("wc: a code that is no number")
        s = mx_ref.live(d["ws"][r])
        if ((s != none) & ((s < least) | (s > most))).any(): b.append("ws: a scale out of range")
        elif (np.abs(decode(pk(d["wc"][r], d["ws"][r]))) > 1).any(): b.append("a number of W beyond 1")
    return b
def sources(s):
    order = np.argsort(-(s[::16] + np.float32(0.0)), axis=1, kind="stable")
    place = np.argsort(order, axis=1, kind="stable")
    kind = 1 * (s[1::16] > 0) + 2 * (s[2::16] > 0) + 4 * (s[3::16] > 0)
    used, j = np.zeros((C, 8), bool), np.arange(C)
    c = np.zeros((8, C), np.int64)
    for g in range(8):
        look = order[g][(place[(g + 1) % 8][:, None] + np.arange(A)) % C]
        new = ~used[j[:, None], kind[g][look]]
        c[g] = look[j, np.argmax(new, axis=1)]
        used[j, kind[g][c[g]]] = True
    return c
def reference(x, u, v, wc, ws):
    qu = [mx_ref.quantize(u[r]) for r in range(N)]
    lay = [[pick(pk(wc[r], ws[r]), np.arange(128 * b, 128 * b + 128)) for b in range(4)] for r in range(N)]
    now = [x[r] for r in range(N)]
    for h in STEP:
        q = [mx_ref.quantize(now[r]) for r in range(N)]
        own = [decode(q[r]) for r in range(N)]
        took = [sources(mx_ref.matmul(qu[r], q[r])) for r in range(N)]
        z = [mx_ref.quantize(gcols(own[r].astype(BF), took[r])) for r in range(N)]
        made = []
        for r in range(N):
            e = r ^ h
            back = mx_ref.quantize(tile([mx_ref.matmul(lay[e][b], z[r]) * np.float32(0.03125) + own[e][:, b::4] for b in range(4)]))
            first = np.full((8, C), -1)
            for g in range(8):
                for j in range(C - 1, -1, -1): first[g, took[r][g, j]] = j
            made.append((own[r] + gcols(decode(back).astype(BF), first).astype(np.float32)).astype(BF))
        now = made
    y, src = np.zeros((N, 128, C), np.float32), np.zeros((N, 8, C), np.float32)
    oc, osc = np.zeros((N, 128, 4 * C), np.uint8), np.zeros((N, 16, C), np.uint8)
    for r in range(N):
        p = mx_ref.quantize(now[r])
        y[r] = mx_ref.matmul(mx_ref.quantize(v[r]), p)
        src[r] = took[r]
        oc[r], osc[r] = emit(p)
    return {"y": y, "src": src, "oc": oc, "osc": osc}

from concourse.bass import DstId, RemoteDMATransfer
from concourse.mybir import dt, AluOpType, AxisListType, ActivationFunctionType

A = AluOpType
F = ActivationFunctionType
STEP = [4, 1]
C = 256
EPS = 2.0 ** -10
LOOK = 14
SLOT = LOOK + 1
NW = SLOT * C

SCRATCH = {}


def _buf(kind, n, *names):
    for s in names:
        if kind == "c":
            SCRATCH["q" + s] = ("sbuf", [128, n], "float8_e4m3fn_x4")
            SCRATCH["s" + s] = ("sbuf", [128, n], "uint8")
        else:
            SCRATCH[s] = ("sbuf", [128, n], {"b": "bfloat16", "f": "float32", "i": "int32", "h": "uint16"}[kind])


_buf("c", 128, "u", "v", "CK")
_buf("c", 144, "M")
_buf("c", 256, "X0", "X1", "X2", "CC", "CA", "B0", "B1", "B2", "B3", "Tc", "Td", "Z", "Y1", "Y2")
_buf("c", 256, "LX1", "LX2", "LY1", "LY2")
_buf("c", 512, "CE", "W")
_buf("c", 1024, "ub")
_buf("b", 1024, "x0", "x1", "x2", "B0", "B1", "B2", "B3", "T1", "CC", "CA", "FX", "FP", "ZT", "YT")
_buf("b", 1040, "DY")
_buf("b", 512, "U", "V", "CK")
_buf("b", 2048, "CE")
_buf("b", 576, "M")
_buf("b", 544, "id2")
_buf("b", 272, "tab", "nc", "dtab")
_buf("b", 256, "m16", "m4", "r16", "r4", "enc", "idr", "ta", "tb", "vk", "ga", "gb")
_buf("b", 128, "tri")
_buf("b", 16, "MK")
_buf("b", NW, "r15", "W1", "WO")
_buf("f", 2048, "T2")
_buf("f", 256, "yo", "so")
_buf("f", 16, "sc", "dl", "nd", "df", "sel", "mm", "poff", "o2f", "cf")
_buf("f", 32, "vb")
_buf("f", 8, "col")
_buf("i", 256, "it")
_buf("i", 64, "ui")
_buf("i", 16, "i1", "i2", "pi")
_buf("h", 64, "uo", "L1", "L2", "LL1", "LL2", "T4")
_buf("h", 16, "offA", "offB", "off2", "slot")
for _k in range(8):
    SCRATCH["P%d" % _k] = ("psum", [128, 512], "float32")

SEMAPHORES = ["eV", "eS", "eT", "eG"]
for _n in ("dx", "du", "dv", "dwc", "dws", "oy0", "oy1", "osr", "oco", "os0", "os1", "os2", "os3"):
    SEMAPHORES.append(_n)
for _h in (1, 2):
    for _n in ("ax", "al", "ay", "lx", "ll", "ly"):
        SEMAPHORES.append(_n + str(_h))


def _overlap(a, b):
    if a[0] >= b[1] or b[0] >= a[1]:
        return False
    if a[2] == b[2] and a[2] > 1 and (a[0] - b[0]) % a[2]:
        return False
    return True


def rank_program(g, core, T, topo):
    rank = T.rank_of(core)
    if rank is None:
        return
    queues = {"V": g.vector, "S": g.scalar, "T": g.tensor, "G": g, "Y": g.sync}
    count = {"V": 0, "S": 0, "T": 0, "G": 0}
    known = {k: {} for k in queues}
    clocks = {}
    log = {}
    total = {}

    def ap(v):
        n, a, b, s = v
        return T[n][:, a:b:s] if s > 1 else T[n][:, a:b]

    def w(name, a=0, b=None, s=1):
        return (name, a, SCRATCH[name][1][1] if b is None else b, s)

    def need(q, sem, val):
        k = known[q]
        if k.get(sem, 0) >= val:
            return
        queues[q].wait_ge(T.sem[sem], val)
        for a, b in clocks.get((sem, val), {}).items():
            if k.get(a, 0) < b:
                k[a] = b
        k[sem] = max(k.get(sem, 0), val)

    def order(q, reads, writes, event):
        waits = {}
        for views, wr in ((reads, False), (writes, True)):
            for v in views:
                psum = SCRATCH[v[0]][0] == "psum"
                for (o, oq, owr, ev) in log.get(v[0], []):
                    if not psum and not _overlap(v[1:], o):
                        continue
                    same = oq == q and q in count
                    if psum:
                        if same and (q == "T" or not owr):
                            continue
                    else:
                        if not wr and not owr:
                            continue
                        if same and not owr:
                            continue
                    waits[ev[0]] = max(waits.get(ev[0], 0), ev[1])
        for sem in sorted(waits):
            need(q, sem, waits[sem])
        for views, wr in ((reads, False), (writes, True)):
            for v in views:
                lst = log.setdefault(v[0], [])
                if wr and v[3] == 1:
                    lst[:] = [e for e in lst if not (v[1] <= e[0][0] and e[0][1] <= v[2])]
                elif not wr:
                    lst[:] = [e for e in lst if e[2] or e[1] != q or e[0] != v[1:] or e[3][0] != event[0]]
                lst.append((v[1:], q, wr, event))
        clocks[event] = dict(known[q])

    def op(q, make, reads, writes):
        count[q] += 1
        ev = ("e" + q, count[q])
        order(q, reads, writes, ev)
        make().then_inc(T.sem[ev[0]], 1)
        total[ev[0]] = ev[1]

    def dma(q, sem, make, reads, writes):
        order(q, reads, writes, (sem, 16))
        make(queues[q]).then_inc(T.sem[sem], 16)
        total[sem] = 16

    def ts(o, i, s1, s2, op0, op1=None, off=None, q=None):
        reads = [i] + [s for s in (s1, s2) if isinstance(s, tuple)] + ([off] if off else [])
        a1 = ap(s1) if isinstance(s1, tuple) else s1
        a2 = ap(s2) if isinstance(s2, tuple) else s2
        src = ap(i).indirect(ap(off)) if off else ap(i)
        if op1 is None:
            op("V", lambda: g.vector.tensor_scalar(ap(o), src, a1, None, op0), reads, [o])
        else:
            op("V", lambda: g.vector.tensor_scalar(ap(o), src, a1, a2, op0, op1), reads, [o])

    def tt(o, a, b, f, off=None):
        src = ap(a).indirect(ap(off)) if off else ap(a)
        op("V", lambda: g.vector.tensor_tensor(ap(o), src, ap(b), f), [a, b] + ([off] if off else []), [o])

    def cp(o, i, off=None, to=None):
        if off:
            op("V", lambda: g.vector.tensor_copy(ap(o), ap(i).indirect(ap(off))), [i, off], [o])
        elif to:
            op("V", lambda: g.vector.tensor_copy(ap(o).indirect(ap(to)), ap(i)), [i, to], [o])
        else:
            op("V", lambda: g.vector.tensor_copy(ap(o), ap(i)), [i], [o])

    def act(o, i, f, bias=None, scale=None, off=None):
        kw = {}
        reads = [i]
        if bias is not None:
            kw["bias"] = ap(bias) if isinstance(bias, tuple) else bias
            if isinstance(bias, tuple):
                reads.append(bias)
        if scale is not None:
            kw["scale"] = ap(scale) if isinstance(scale, tuple) else scale
            if isinstance(scale, tuple):
                reads.append(scale)
        src = ap(i).indirect(ap(off)) if off else ap(i)
        if off:
            reads.append(off)
        op("S", lambda: g.scalar.activation(ap(o), src, f, **kw), reads, [o])

    def fill(o, c):
        op("V", lambda: g.vector.memset(ap(o), c), [], [o])

    def scan(o, d0, d1, init, f0, f1):
        op("V", lambda: g.vector.tensor_tensor_scan(ap(o), ap(d0), ap(d1), init, f0, f1), [d0, d1], [o])

    def quant(name, i, a=0, b=None):
        qo, so = w("q" + name, a, b), w("s" + name, a, b)
        op("V", lambda: g.vector.quantize_mx(ap(qo), ap(so), ap(i)), [i], [qo, so])

    def mm(out, n, lhs, la, rhs, ra, start=True, stop=True):
        o = w(out, 0, n)
        l1, l2 = w("q" + lhs, la, la + 128), w("s" + lhs, la, la + 128)
        r1, r2 = w("q" + rhs, ra, ra + n), w("s" + rhs, ra, ra + n)
        op("T", lambda: g.tensor.matmul_mx(ap(o), ap(l1), ap(l2), ap(r1), ap(r2), start, stop), [l1, l2, r1, r2], [o])

    def iota(o, pattern, base, cm):
        small = SCRATCH[o[0]][2] == "bfloat16"
        if small:
            op("G", lambda: g.iota(ap(o), pattern, base, cm, allow_small_or_imprecise_dtypes=True), [], [o])
        else:
            op("G", lambda: g.iota(ap(o), pattern, base, cm), [], [o])

    def affine(o, pattern, cond, const, base, cm):
        op("G", lambda: g.affine_select(ap(o), ap(o), pattern, cond, const, base, cm), [o], [o])

    def send(dst, parts, rsem, lsem):
        rid, pid = topo.addr(dst, core)
        mask = topo.mask(core, dst)
        eng = len(topo.engines(core, dst))
        for k, (o, i) in enumerate(parts):
            order("G", [i], [], (lsem, eng * len(parts)))
            codes = SCRATCH[o[0]][2] == "float8_e4m3fn_x4"
            g.remote_dma(ap(o).bitcast(dt.uint8) if codes else ap(o), ap(i).bitcast(dt.uint8) if codes else ap(i),
                         T.sem[rsem], T.sem[lsem], pid, rid, mask)
        total[lsem] = eng * len(parts)

    def arrive(src, views, parts, rsem):
        n = len(topo.engines(src, core)) * parts
        for v in views:
            log.setdefault(v[0], []).append((v[1:], "R", True, (rsem, n)))
        total[rsem] = n

    dma("Y", "dx", lambda e: e.dma_start(ap(w("x0")), T.x[:]), [], [w("x0")])
    dma("S", "du", lambda e: e.dma_start(ap(w("U")), T.u[:]), [], [w("U")])
    dma("Y", "dwc", lambda e: e.dma_start(ap(w("qW")).bitcast(dt.uint8), T.wc[:]), [], [w("qW")])
    dma("S", "dv", lambda e: e.dma_start(ap(w("V")), T.v[:]), [], [w("V")])
    dma("Y", "dws", lambda e: e.dma_start(ap(w("sW")), T.ws[:]), [], [w("sW")])

    iota(w("ui"), [[16, 8], [0, 8]], 0, 0)
    fill(w("tri"), 0.0)
    fill(w("CE"), 0.0)
    fill(w("CK"), 0.0)
    cp(w("uo"), w("ui"))
    affine(w("tri"), [[-1, 128]], A.is_ge, 1.0, 0, 1)
    for b in range(4):
        affine(w("CE", 512 * b + b, 512 * b + 512, 4), [[-1, 128]], A.not_equal, 32.0, 0, 1)
    for i, c in ((1, 1.0), (2, 2.0), (3, 4.0)):
        affine(w("CK", 0, 512, 4), [[-16, 8], [0, 16]], A.not_equal, c, -i, 1)
    fill(w("T1"), 0.0)
    fill(w("CC"), 0.0)
    for a, e in ((112, 0), (112, 1), (128, 2), (128, 3), (240, 0), (240, 1)):
        fill(w("CC", 4 * a + e, 4 * a + 64, 4), 1.0)
    quant("CC", w("CC"))
    quant("CE", w("CE"))
    quant("CK", w("CK"))

    quant("u", w("U"))
    quant("X0", w("x0"))
    for k in range(4):
        qo, so = w("qub", 256 * k, 256 * k + 256), w("sub", 256 * k, 256 * k + 256)
        of = w("uo", 16 * k, 16 * k + 16)
        op("V", lambda: g.vector.tensor_copy(ap(qo).bitcast(dt.uint32), T["qu"][:, 0:128].bitcast(dt.uint32).indirect(ap(of))), [w("qu"), of], [qo])
        op("S", lambda: g.scalar.activation(ap(so), T["su"][:, 0:128].indirect(ap(of)), F.Copy), [w("su"), of], [so])

    def late_pool():
        fill(w("MK"), LOOK * EPS)
        iota(w("it"), [[1, C]], 128, -1)
        iota(w("pi", 0, 2), [[0, 2]], 0, 1)
        iota(w("idr"), [[1, C]], 1, 0)
        iota(w("enc"), [[-1, C]], C, 0)
        affine(w("MK", 0, 8), [[-16, 8]], A.is_ge, 0.0, 0, 1)
        affine(w("MK", 0, 8), [[16, 8]], A.is_ge, 0.0, 15, -1)

    def late_vector():
        ts(w("it"), w("it"), 15, None, A.bitwise_and)
        ts(w("m16"), w("it"), 0.0, None, A.is_equal)
        iota(w("it"), [[4, C]], 131, -1)
        fill(w("r16"), 1.0)
        fill(w("r16", 0, C, 16), 0.0)
        fill(w("r4"), 1.0)
        fill(w("r4", 0, C, 4), 0.0)
        ts(w("it"), w("it"), 15, None, A.bitwise_and)
        ts(w("m4"), w("it"), 4.0, None, A.is_lt)
        ts(w("i1", 0, 2), w("pi", 0, 2), 7, None, A.bitwise_and)
        ts(w("i2", 0, 2), w("pi", 0, 2), 3, None, A.bitwise_and)
        ts(w("col", 0, 1), w("i1", 0, 1), -1.0, None, A.mult)
        ts(w("col", 1, 2), w("i2", 0, 1), -4.0, None, A.add)
        ts(w("col", 2, 3), w("i2", 0, 1), 1024.0, None, A.add)
        fill(w("vb"), (LOOK - 0.5) * EPS)

    def last_vector():
        fill(w("CA"), 0.0)
        fill(w("M"), 0.0)
        fill(w("id2"), 0.0)
        fill(w("DY", 1024, 1040), 0.0)
        for gg in range(8):
            a = 512 * (gg // 4) + 64 * gg + gg % 4
            act(w("CA", a, a - gg % 4 + 64, 4), w("m16", 0, 16), F.Copy, scale=2.0 / EPS)
        quant("CA", w("CA"))
        quant("v", w("V"))

    late_pool()

    for h in (1, 2):
        mate = T.cores[rank ^ STEP[h - 1]]
        X, XN = "X%d" % (h - 1), "X%d" % h
        LX, LY, Y, L, LL = "LX%d" % h, "LY%d" % h, "Y%d" % h, "L%d" % h, "LL%d" % h
        R = lambda s: "%s%d" % (s, h)

        mm("P1", 128, X, 0, "u", 0)
        mm("P2", 128, X, 128, "u", 0)
        for gg in range(4):
            mm("P%d" % (3 + gg), C, "ub", 128 * gg, X, 0)
        mm("P0", C, "u", 0, X, 0)
        send(mate, [(w("q" + LX), w("q" + X)), (w("s" + LX), w("s" + X))], R("ax"), R("lx"))
        arrive(mate, [w("q" + LX), w("s" + LX)], 2, R("ax"))
        iota(w("W1"), [[0, NW]], 0, 0)

        for k in range(2):
            cp(w("sc", 8 * k, 8 * k + 8), w("P%d" % (1 + k), 0, 128, 16))
        for k in range(2):
            act(w("dl", 8 * k, 8 * k + 8), w("P%d" % (1 + k), 0, 128, 16), F.Abs, scale=0.625 * 2.0 ** -23)
        ts(w("dl"), w("dl"), 2.0 ** -118, None, A.max)
        tt(w("nd"), w("sc"), w("dl"), A.subtract)
        tt(w("df"), w("sc"), w("nd"), A.subtract)

        def thresholds(gg):
            for k in range(2):
                j = 8 * k + gg
                act(w("T2", 256 * gg + 128 * k, 256 * gg + 128 * k + 128), w("tri"), F.Identity, bias=w("nd", j, j + 1), scale=w("df", j, j + 1))

        def compares(gg):
            P, B, e = "P%d" % (3 + gg % 4), "B%d" % (gg // 2), 2 * (gg % 2)
            ts(w(B, 512 + e, 1024, 4), w(P, 128, 256), w("sc", gg, gg + 1), None, A.is_le)
            ts(w(B, e + 1, 512, 4), w(P, 0, 128), w("sc", 8 + gg, 9 + gg), None, A.is_lt)
            tt(w(B, e, 512, 4), w(P, 0, 128), w("T2", 256 * gg, 256 * gg + 128), A.is_le)
            tt(w(B, 512 + e + 1, 1024, 4), w(P, 128, 256), w("T2", 256 * gg + 128, 256 * gg + 256), A.is_le)

        def counts(G):
            mm("P0", C, "CC", 112 - 32 * G, "B%d" % G, 0, G == 0, G == 3)
            mm("P1", C, "CC", 128 - 32 * G, "B%d" % G, 0, G == 0, G == 3)

        thresholds(0)
        thresholds(1)
        act(w("ta"), w("P0", 0, C), F.Sign)
        act(w("T1", 0, 1024, 4), w("ta"), F.Relu)
        compares(0)
        mm("P3", C, "ub", 128 * 4, X, 0)
        compares(1)
        mm("P4", C, "ub", 128 * 5, X, 0)
        quant("B0", w("B0"))
        quant("Tc", w("T1"))
        mm("P7", C, "CK", 0, "Tc", 0)
        counts(0)
        thresholds(2)
        thresholds(3)
        compares(2)
        mm("P5", C, "ub", 128 * 6, X, 0)
        compares(3)
        mm("P6", C, "ub", 128 * 7, X, 0)
        if h == 1:
            late_vector()
        quant("B1", w("B1"))
        counts(1)
        act(w("ta"), w("P7", 0, C), F.Abs, bias=w("col", 0, 1))
        act(w("tb"), w("ta"), F.Sign, bias=-0.5)
        thresholds(4)
        thresholds(5)
        thresholds(6)
        thresholds(7)
        compares(4)
        compares(5)
        quant("B2", w("B2"))
        counts(2)
        tt(w("vk"), w("tb"), w("idr"), A.mult)
        compares(6)
        compares(7)
        quant("B3", w("B3"))
        counts(3)
        tt(w("ga"), w("P0", 0, C), w("m16"), A.mult)
        tt(w("gb"), w("P1", 0, C), w("m16"), A.mult)
        scan(w("ta"), w("r16"), w("ga"), 0.0, A.mult, A.add)
        scan(w("tb"), w("r16"), w("gb"), 0.0, A.mult, A.add)
        ts(w("offA"), w("ta", 15, C, 16), -1.0, 269.0, A.mult, A.add)
        ts(w("offB"), w("tb", 15, C, 16), -1.0, 269.0, A.mult, A.add)
        if h == 1:
            fill(w("tab", 0, 272), 0.0)
        cp(w("tab", 0, 270), w("vk"), to=w("offA"))
        ts(w("poff"), w("tb", 15, C, 16), -2.0, 510.0, A.mult, A.add)
        cp(w("tab", 0, 14), w("tab", 256, 270))
        ts(w("nc", 0, 270), w("tab", 0, 270), 0.0, None, A.is_gt)
        scan(w("dtab", 0, 270), w("nc", 0, 270), w("nc", 0, 270), 64.0, A.mult, A.add)
        ts(w("T1", 0, 1024, 4), w("dtab", 0, 270), EPS / 32.0, None, A.mult, off=w("offB"))
        quant("Td", w("T1"))
        if h == 1:
            last_vector()

        for b in range(4):
            mm("P%d" % (3 + b), C, "CE", 128 * b, X, 0)
        for b in range(4):
            act(w("FX", b, 1024, 4), w("P%d" % (3 + b), 0, C), F.Copy, scale=0.03125)
        act(w("id2", 0, 540, 2), w("tab", 0, 270), F.Abs)
        act(w("id2", 1, 513, 2), w("tab", 14, 270), F.Abs)
        mm("P2", 128, "Td", 0, "CE", 0)
        mm("P7", 128, "Td", 128, "CE", 0)
        for b in range(4):
            mm("P%d" % (3 + b), C, "CE", 128 * b, LX, 0)
        for b in range(4):
            act(w("FP", b, 1024, 4), w("P%d" % (3 + b), 0, C), F.Copy, scale=0.03125)
        for b in range(4):
            mm("P%d" % (3 + b), C, "CE", 128 * b, X, 0, True, False)

        D = ["P2", "P7"]
        for k in range(2):
            cp(w("vb", 16 * k, 16 * k + 8), w(D[k], 0, 8))
        for gg in range(8):
            for k in range(2):
                m, v = w("mm", 2 * gg + k, 2 * gg + k + 1), w("vb", 16 * k, 16 * k + 9)
                op("V", lambda: g.vector.tensor_reduce(ap(m), ap(v), AxisListType.X, A.min, negate=True, apply_absolute_value=True), [v], [m])
            if gg < 7:
                for k in range(2):
                    ts(w("sel", 8 * k, 8 * k + 8), w("vb", 16 * k, 16 * k + 8), w("mm", 2 * gg + k, 2 * gg + k + 1), 0.0, A.add, A.is_le)
                for k in range(2):
                    tt(w("vb", 16 * k, 16 * k + 8), w(D[k], 16 * gg + 16, 16 * gg + 24), w("sel", 8 * k, 8 * k + 8), A.subtract)
            for k in range(2):
                a = 4 * (16 * (gg // 4) + 8 * k) + gg % 4
                act(w("M", a, a - gg % 4 + 32, 4), w("MK", 0, 8), F.Relu, bias=w("mm", 2 * gg + k, 2 * gg + k + 1))
        quant("M", w("M"))
        mm("P0", 128, "CA", 0, "M", 0, True, False)
        mm("P0", 128, "CA", 128, "M", 16, False, True)
        tt(w("o2f"), w("P0", 0, 16), w("poff"), A.add)
        cp(w("off2"), w("o2f"))
        tt(w("ga"), w("id2", 0, 540), w("m4"), A.mult, off=w("off2"))
        scan(w("ta"), w("r4"), w("ga"), 0.0, A.mult, A.add)
        ts(w(L), w("ta", 3, C, 4), 4.0, w("col", 1, 2), A.mult, A.add)
        send(mate, [(w(LL), w(L))], R("al"), R("ll"))
        arrive(mate, [w(LL)], 1, R("al"))

        tt(w("gb"), w("id2", 0, 540), w("m16"), A.mult, off=w("off2"))
        cp(w("i1"), w("P0", 0, 16))
        scan(w("tb"), w("r16"), w("gb"), 0.0, A.mult, A.add)
        ts(w("i2"), w("i1"), 1, None, A.arith_shift_right)
        ts(w("cf"), w("tb", 15, C, 16), float(SLOT), float(-SLOT), A.mult, A.add)
        tt(w("cf"), w("cf"), w("i2"), A.add)
        cp(w("slot"), w("cf"))
        cp(w("W1"), w("enc"), to=w("slot"))

        cp(w("ZT", 0, 512), w("FP"), off=w(LL, 0, 32))
        act(w("ZT", 512, 1024), w("FP"), F.Copy, off=w(LL, 32, 64))
        quant("Z", w("ZT"))
        for b in range(4):
            mm("P%d" % (3 + b), C, "W", 128 * b, "Z", 0, False, True)
        for b in (0, 2, 1, 3):
            o, i = w("YT", b, 1024, 4), w("P%d" % (3 + b), 0, C)
            if b < 2:
                ts(o, i, 0.03125, None, A.mult)
            else:
                act(o, i, F.Copy, scale=0.03125)
        quant(Y, w("YT"))
        send(mate, [(w("q" + LY), w("q" + Y)), (w("s" + LY), w("s" + Y))], R("ay"), R("ly"))
        arrive(mate, [w("q" + LY), w("s" + LY)], 2, R("ay"))
        if h == 2:
            act(w("so"), w("id2", 0, 540), F.Identity, bias=-1.0, off=w("off2"))
            dma("Y", "osr", lambda e: e.dma_start(T.src[:], T["so"][0:128:16, :]), [w("so")], [])

        if h == 1:
            fill(w("r15"), 1.0)
            fill(w("r15", 0, NW, SLOT), 0.0)
        scan(w("WO"), w("r15"), w("W1"), 0.0, A.mult, A.max)
        tt(w("gb"), w("WO", SLOT - 1, NW, SLOT), w("m4"), A.mult)
        scan(w("tb"), w("r4"), w("gb"), 0.0, A.mult, A.add)
        ts(w("T4"), w("tb", 3, C, 4), -4.0, w("col", 2, 3), A.mult, A.add)

        for b in range(4):
            mm("P%d" % (3 + b), C, "CE", 128 * b, LY, 0)
        for b in range(4):
            o, i = w("DY", b, 1024, 4), w("P%d" % (3 + b), 0, C)
            if b % 2:
                act(o, i, F.Copy, scale=0.03125)
            else:
                ts(o, i, 0.03125, None, A.mult)
        tt(w("x%d" % h), w("DY", 0, 1040), w("FX"), A.add, off=w("T4"))
        quant(XN, w("x%d" % h))

    mm("P0", C, "v", 0, "X2", 0)
    dma("Y", "oco", lambda e: e.dma_start(T.oc[:], ap(w("qX2")).bitcast(dt.uint8)), [w("qX2")], [])
    for k in range(4):
        dma("S" if k % 2 else "Y", "os%d" % k, lambda e: e.dma_start(T.osc[4 * k:4 * k + 4, :], T["sX2"][32 * k:32 * k + 4, :]), [w("sX2")], [])
    cp(w("yo"), w("P0", 0, C))
    dma("Y", "oy0", lambda e: e.dma_start(T.y[:], ap(w("yo"))), [w("yo")], [])
    for sem in sorted(total):
        if known["G"].get(sem, 0) < total[sem]:
            g.wait_ge(T.sem[sem], total[sem])
